import numpy as np
import ml_dtypes


def mxq(x, axis, fmt="e4m3"):
    dtype, down = {"e4m3": (ml_dtypes.float8_e4m3fn, 7), "e5m2": (ml_dtypes.float8_e5m2, 14)}[fmt]
    v = np.moveaxis(np.asarray(x, np.float32).astype(ml_dtypes.bfloat16).astype(np.float64), axis, -1)
    blocks = v.reshape(v.shape[:-1] + (-1, 32))
    amax = np.abs(blocks).max(-1, keepdims=True)
    byte = np.maximum(np.where(amax > 0, np.frexp(amax)[1] - 1 + 127, 0) - down, 1)
    scale = np.exp2(byte - 127.0)
    codes = (blocks / scale).astype(np.float32).astype(dtype).astype(np.float64)
    return np.moveaxis((codes * scale).reshape(v.shape), -1, axis)


WIDE = False


def mx_kscale(k):
    if not WIDE:
        return np.ones(k)
    levels = np.array([10, -10, 5, -5, 0])
    if k % 512:
        return np.exp2(np.random.permutation(np.resize(levels, k // 32))).repeat(32)
    a = np.empty((k // 512, 16))
    for p in range(k // 512):
        a[p, :8] = np.random.permutation(np.resize(levels, 8))
        for g in range(8):
            far = levels[np.abs(levels - a[p, g]) >= 10]
            a[p, g + 8] = far[np.random.randint(len(far))]
    return np.exp2(a.ravel()).repeat(32)


def f64(x):
    return np.asarray(x).astype(np.float64)


def striped(idx):
    return np.tile(idx.reshape(-1, 16).T, (8, 1)).astype(np.uint16)


def unstriped(offs):
    return offs[:16].T.reshape(-1).astype(np.int64)


E2M1 = np.array([0.0, 0.5, 1.0, 1.5, 2.0, 3.0, 4.0, 6.0, -0.0, -0.5, -1.0, -1.5, -2.0, -3.0, -4.0, -6.0])


def pack_weight(w, fmt):
    k, n = w.shape
    w = f64(np.asarray(w, np.float32).astype(ml_dtypes.bfloat16)).reshape(k // 32, 32, n)
    amax = np.abs(w).max(1)
    if fmt == "e4m3":
        byte = np.frexp(amax)[1] - 1 + 127 - 7
    else:
        mant, ex = np.frexp(amax / 6.0)
        byte = np.where(mant > 0.5, ex, ex - 1) + 127
    byte = np.clip(np.where(amax > 0, byte, 1), 1, 254)
    scaled = (w * np.exp2(127.0 - byte)[:, None, :]).reshape(k, n).astype(np.float32)
    by_word = np.ascontiguousarray(scaled.reshape(k // 512, 128, 4, n).transpose(0, 1, 3, 2))
    if fmt == "e4m3":
        words = by_word.astype(ml_dtypes.float8_e4m3fn).view(np.uint8)
    else:
        c = by_word.astype(ml_dtypes.float4_e2m1fn).view(np.uint8) & 0xF
        words = (c[..., 0::2] | (c[..., 1::2] << 4)).reshape(k // 512, 128, 2 * n)
    return np.ascontiguousarray(words), np.ascontiguousarray(byte.astype(np.uint8).reshape(k // 512, 16, n))


def unpack_weight(words, scales, fmt):
    g, _, n = scales.shape
    words = np.ascontiguousarray(words).reshape(g, 128, n, -1)
    if fmt == "e4m3":
        vals = words.view(ml_dtypes.float8_e4m3fn).astype(np.float64)
    else:
        nib = np.empty((g, 128, n, 4), np.uint8)
        nib[..., 0::2] = words & 0xF
        nib[..., 1::2] = words >> 4
        vals = E2M1[nib]
    vals = vals * np.repeat(np.exp2(scales.astype(np.float64) - 127.0), 8, axis=1)[..., None]
    return vals.transpose(0, 1, 3, 2).reshape(g * 512, n)


def gelu(v):
    return 0.5 * v * (1.0 + np.tanh(np.sqrt(2.0 / np.pi) * (v + 0.044715 * v**3)))


K, K2, H, N, T, S = 1024, 512, 1024, 384, 4096, 1024


def setup_inputs():
    n = np.random.standard_normal
    s = mx_kscale(K)[:, None]
    s2 = mx_kscale(K2)[:, None]
    u = mx_kscale(H)[:, None]
    d = {}
    d["tab_words"], d["tab_scales"] = pack_weight(n((K, T)) * s, "e4m3")
    d["offs"] = striped(np.random.permutation(T)[:S])
    d["xs_words"], d["xs_scales"] = pack_weight(n((K2, S)) * s2, "e4m3")
    d["w1"] = (1.4 * n((K, H)) / s / K ** 0.5).astype(np.float32)
    d["b1"] = (0.6 * n(H)).astype(np.float32)
    d["w2"] = (n((K2, H)) / s2 * u.T / K2 ** 0.5).astype(np.float32)
    d["w3"] = (n((K, N)) / s / K ** 0.5).astype(np.float32)
    d["b3"] = (0.6 * n(N)).astype(np.float32)
    d["w4_words"], d["w4_scales"] = pack_weight(1.4 * n((H, N)) / u / H ** 0.5, "e2m1")
    return d


def reference(tab_words, tab_scales, offs, xs_words, xs_scales, w1, b1, w2, w3, b3, w4_words, w4_scales):
    v = unpack_weight(tab_words, tab_scales, "e4m3")[:, unstriped(offs)]
    xs = unpack_weight(xs_words, xs_scales, "e4m3")
    w4 = unpack_weight(w4_words, w4_scales, "e2m1")
    expect = np.tanh((mxq(f64(w1), 0, "e4m3").T @ v) + f64(b1)[:, None])
    sung = mxq(f64(w2), 0, "e4m3").T @ xs
    h = expect * sung
    y = w4.T @ mxq(h, 0, "e4m3")
    base = (mxq(f64(w3), 0, "e4m3").T @ v) + f64(b3)[:, None]
    return np.maximum(y, base)

@@ -1,0 +1,244 @@
+from contextlib import ExitStack
+
+import concourse.mybir as mybir
+
+K, K2, H, N, T, S = 1024, 512, 1024, 384, 4096, 1024
+FLOPS = 2 * S * (K * H + K2 * H + H * N + K * N)
+
+F32 = mybir.dt.float32
+BF16 = mybir.dt.bfloat16
+I32 = mybir.dt.int32
+U32 = mybir.dt.uint32
+U16 = mybir.dt.uint16
+U8 = mybir.dt.uint8
+FP8X4 = mybir.dt.float8_e4m3fn_x4
+FP4X4 = mybir.dt.float4_e2m1fn_x4
+ACT = mybir.ActivationFunctionType
+ALU = mybir.AluOpType
+
+P = 128
+PACK = 4
+PASS = P * PACK
+BANK = 512
+HALVES = S // BANK
+K_PASSES = K // PASS
+H_PASSES = H // PASS
+N_TILES = N // P
+CHUNK = BANK // PACK
+
+
+def tile_list_karaoke_passage_scorer_kernel(
+    tc, tab_words, tab_scales, offs, xs_words, xs_scales, w1, b1, w2, w3, b3, w4_words, w4_scales, out
+):
+    nc = tc.nc
+    with ExitStack() as ctx:
+        keep = ctx.enter_context(tc.tile_pool(name="keep", bufs=1))
+        ring = ctx.enter_context(tc.tile_pool(name="ring", bufs=1))
+        psum = ctx.enter_context(tc.psum_pool(name="psum", bufs=8))
+
+        offsets = keep.tile([P, S // 16], U16, name="offsets")
+
+        def load_rows(name, rows):
+            width = rows.shape[1]
+            raw = keep.tile([P, PACK, width], F32, name=name)
+            nc.sync.dma_start(out=raw[:], in_=rows.rearrange("(p j) w -> p j w", j=PACK))
+            return raw
+
+        def load_words(name, words):
+            tile = keep.tile([P, words.shape[1]], I32, name=name, align_bytes=64)
+            nc.sync.dma_start(out=tile[:], in_=words.rearrange("p c i -> p (c i)").bitcast(I32))
+            return tile
+
+        def w1_rows(a, b):
+            return w1[a * PASS : (a + 1) * PASS, b * PASS : (b + 1) * PASS]
+
+        def load_plane(name, scales, side_by_side):
+            passes, width = scales.shape[0], scales.shape[2]
+            plane = keep.tile([P, passes * width if side_by_side else width], U8, name=name, align_bytes=64)
+            nc.vector.memset(plane[:].bitcast(I32), 0)
+            for q in range(4):
+                rows = scales[:, 4 * q : 4 * q + 4, :].bitcast(I32)
+                if side_by_side:
+                    nc.sync.dma_start(
+                        out=plane[32 * q : 32 * q + 4, :].bitcast(I32).rearrange("r (b c) -> r b c", b=passes),
+                        in_=rows.rearrange("b r c -> r b c"),
+                    )
+                else:
+                    nc.sync.dma_start(out=plane[32 * q : 32 * q + 4 * passes, :].bitcast(I32), in_=rows)
+            return plane
+
+        w1_raw, w2_raw, w3_raw, table = {}, {}, {}, {}
+        w1_raw[0, 0] = load_rows("w1_raw00", w1_rows(0, 0))
+        table_scales = load_plane("table_scales", tab_scales, False)
+        nc.sync.dma_start(offsets[:], offs)
+        table[0] = load_words("table0", tab_words[0])
+        w1_raw[1, 0] = load_rows("w1_raw10", w1_rows(1, 0))
+        bias1 = keep.tile([P, H_PASSES, PACK], F32, name="bias1")
+        nc.sync.dma_start(out=bias1[:], in_=b1.rearrange("(b p t) -> p b t", p=P, t=PACK))
+        table[1] = load_words("table1", tab_words[1])
+        w2_raw[0] = load_rows("w2_raw0", w2[:, 0:PASS])
+        xs_plane = load_plane("xs_plane", xs_scales, False)
+        xs = load_words("xs", xs_words[0])
+        w1_raw[0, 1] = load_rows("w1_raw01", w1_rows(0, 1))
+        w1_raw[1, 1] = load_rows("w1_raw11", w1_rows(1, 1))
+        w2_raw[1] = load_rows("w2_raw1", w2[:, PASS : 2 * PASS])
+        for a in range(K_PASSES):
+            w3_raw[a] = load_rows("w3_raw%d" % a, w3[a * PASS : (a + 1) * PASS, :])
+        bias3 = keep.tile([P, N_TILES], F32, name="bias3")
+        with nc.allow_non_contiguous_dma(reason="one bias value to a partition"):
+            nc.sync.dma_start(out=bias3[:], in_=b3.rearrange("(c p) -> p c", p=P))
+        w4 = keep.tile([P, H_PASSES, 2 * N], U8, name="w4", align_bytes=64)
+        nc.sync.dma_start(out=w4[:].bitcast(I32), in_=w4_words.bitcast(I32).rearrange("b p c -> p b c"))
+        w4_plane = load_plane("w4_plane", w4_scales, True)
+
+        def copy_on(engine):
+            return nc.scalar.copy if engine == "scalar" else nc.vector.tensor_copy
+
+        def round_dealt(raw, engine):
+            grouped = ring.tile([P, PACK * P * PACK], BF16, name="grouped", bufs=4, align_bytes=64)
+            copy_on(engine)(
+                out=grouped[:].rearrange("p (t m j) -> p m j t", t=PACK, j=PACK),
+                in_=raw[:].rearrange("p j (m t) -> p m j t", t=PACK),
+            )
+            return grouped
+
+        def round_plain(raw, engine):
+            grouped = ring.tile([P, PACK * P * PACK], BF16, name="grouped", bufs=4, align_bytes=64)
+            copy_on(engine)(
+                out=grouped[:, 0 : N * PACK].rearrange("p (c i j) -> p c j i", i=4, j=PACK),
+                in_=raw[:].rearrange("p j (c i) -> p c j i", i=4),
+            )
+            return grouped
+
+        def quantise(name, grouped, widths):
+            columns = sum(widths)
+            codes = keep.tile([P, columns], U32, name=name + "_codes", align_bytes=64)
+            plane = keep.tile([P, columns], U8, name=name + "_plane", align_bytes=64)
+            c0 = 0
+            for width in widths:
+                nc.vector.quantize_mx(
+                    out=codes[:, c0 : c0 + width].bitcast(FP8X4),
+                    scales=plane[:, c0 : c0 + width],
+                    in_=grouped[:, PACK * c0 : PACK * (c0 + width)],
+                )
+                c0 += width
+            return codes, plane
+
+        def gather(name, dtype, window, u):
+            picked = keep.tile([P, BANK], dtype, name=name, align_bytes=64)
+            columns = BANK // 16
+            nc.vector.tensor_copy(picked[:], window.indirect(offsets[:, u * columns : (u + 1) * columns]))
+            return picked
+
+        def table_pass(acc, weight, col0, a, u):
+            codes, plane = weight
+            nc.tensor.matmul_mx(
+                out=acc[:],
+                lhsT=codes[:, col0 : col0 + P].bitcast(FP8X4),
+                lhsT_scale=plane[:, col0 : col0 + P],
+                rhs=v_words[a, u][:].bitcast(FP8X4),
+                rhs_scale=v_plane[u][4 * a : P, :],
+                start=(a == 0),
+                stop=(a == K_PASSES - 1),
+            )
+
+        def new_bank():
+            return psum.tile([P, BANK], F32, name="bank")
+
+        def bound(b, banks):
+            expect = ring.tile([P, PACK, BANK], F32, name="expect", bufs=3)
+            for t in range(PACK):
+                nc.scalar.activation(
+                    out=expect[:, t, :], in_=banks[t][:], func=ACT.Tanh, bias=bias1[:, b, t : t + 1]
+                )
+            return expect
+
+        def times_sung(b, u, expect):
+            codes, plane = w2_mx[b]
+            h_rounded = ring.tile([P, BANK * PACK], BF16, name="h_rounded", bufs=2, align_bytes=64)
+            for c in range(PACK):
+                sung = new_bank()
+                s0 = u * BANK + c * CHUNK
+                for t in range(PACK):
+                    nc.tensor.matmul_mx(
+                        out=sung[:, t * CHUNK : (t + 1) * CHUNK],
+                        lhsT=codes[:, t * P : (t + 1) * P].bitcast(FP8X4),
+                        lhsT_scale=plane[:, t * P : (t + 1) * P],
+                        rhs=xs[:, s0 : s0 + CHUNK].bitcast(FP8X4),
+                        rhs_scale=xs_plane[:, s0 : s0 + CHUNK],
+                        start=True,
+                        stop=True,
+                    )
+                nc.vector.tensor_tensor(
+                    out=h_rounded[:, c * BANK : (c + 1) * BANK].rearrange("p (g i t) -> p g t i", i=4, t=PACK),
+                    in0=sung[:].rearrange("p (t g i) -> p g t i", t=PACK, i=4),
+                    in1=expect[:, :, c * CHUNK : (c + 1) * CHUNK].rearrange("p t (g i) -> p g t i", i=4),
+                    op=ALU.mult,
+                )
+            return h_rounded
+
+        v_words, v_plane, w1_mx, w2_mx, w3_mx, h_mx = {}, {}, {}, {}, {}, {}
+        for u in range(HALVES):
+            v_plane[u] = gather("v_plane%d" % u, U8, table_scales[:], u)
+        w1_mx[0, 0] = quantise("w1_00", round_dealt(w1_raw[0, 0], "scalar"), [PASS])
+        for u in range(HALVES):
+            v_words[0, u] = gather("v_words0%d" % u, U32, table[0][:].bitcast(U32), u)
+        banks = {}
+        for u in range(HALVES):
+            for t in range(PACK):
+                banks[u, t] = new_bank()
+                table_pass(banks[u, t], w1_mx[0, 0], t * P, 0, u)
+        w1_mx[1, 0] = quantise("w1_10", round_dealt(w1_raw[1, 0], "scalar"), [PASS])
+        expect = {}
+        for u in range(HALVES):
+            v_words[1, u] = gather("v_words1%d" % u, U32, table[1][:].bitcast(U32), u)
+            for t in range(PACK):
+                table_pass(banks[u, t], w1_mx[1, 0], t * P, 1, u)
+            expect[0, u] = bound(0, [banks[u, t] for t in range(PACK)])
+        w2_mx[0] = quantise("w2_0", round_dealt(w2_raw[0], "vector"), [PASS])
+        w1_grouped = round_dealt(w1_raw[0, 1], "scalar")
+        h_rounded = times_sung(0, 0, expect[0, 0])
+        w1_mx[0, 1] = quantise("w1_01", w1_grouped, [PASS])
+        h_mx[0, 0] = quantise("h_00", h_rounded, [BANK])
+        w1_grouped = round_dealt(w1_raw[1, 1], "scalar")
+        h_rounded = times_sung(0, 1, expect[0, 1])
+        w1_mx[1, 1] = quantise("w1_11", w1_grouped, [PASS])
+        h_mx[0, 1] = quantise("h_01", h_rounded, [BANK])
+        w2_mx[1] = quantise("w2_1", round_dealt(w2_raw[1], "vector"), [PASS])
+        for u in range(HALVES):
+            for t in range(PACK):
+                banks[u, t] = new_bank()
+                for a in range(K_PASSES):
+                    table_pass(banks[u, t], w1_mx[a, 1], t * P, a, u)
+            expect[1, u] = bound(1, [banks[u, t] for t in range(PACK)])
+        w3_mx[0] = quantise("w3_0", round_plain(w3_raw[0], "vector"), [256, 128])
+        h_rounded = times_sung(1, 0, expect[1, 0])
+        w3_mx[1] = quantise("w3_1", round_plain(w3_raw[1], "scalar"), [256, 128])
+        h_mx[1, 0] = quantise("h_10", h_rounded, [BANK])
+        h_rounded = times_sung(1, 1, expect[1, 1])
+        base = {}
+        for u in range(HALVES):
+            for n in range(N_TILES):
+                acc = new_bank()
+                for a in range(K_PASSES):
+                    table_pass(acc, w3_mx[a], n * P, a, u)
+                base[u, n] = keep.tile([P, BANK], F32, name="base%d%d" % (u, n))
+                nc.scalar.activation(out=base[u, n][:], in_=acc[:], func=ACT.Identity, bias=bias3[:, n : n + 1])
+        h_mx[1, 1] = quantise("h_11", h_rounded, [BANK])
+        for u in range(HALVES):
+            for n in range(N_TILES):
+                acc = new_bank()
+                for b in range(H_PASSES):
+                    codes, plane = h_mx[b, u]
+                    nc.tensor.matmul_mx(
+                        out=acc[:],
+                        lhsT=w4[:, b, 2 * n * P : 2 * (n + 1) * P].bitcast(FP4X4),
+                        lhsT_scale=w4_plane[:, b * N + n * P : b * N + (n + 1) * P],
+                        rhs=codes[:].bitcast(FP8X4),
+                        rhs_scale=plane[:],
+                        start=(b == 0),
+                        stop=(b == H_PASSES - 1),
+                    )
+                score = keep.tile([P, BANK], F32, name="score%d%d" % (u, n))
+                nc.vector.tensor_tensor(out=score[:], in0=acc[:], in1=base[u, n][:], op=ALU.max)
+                nc.sync.dma_start(out=out[n * P : (n + 1) * P, u * BANK : (u + 1) * BANK], in_=score[:])

@@ -34,7 +34,7 @@ def tile_list_karaoke_passage_scorer_kernel(
     with ExitStack() as ctx:
         keep = ctx.enter_context(tc.tile_pool(name="keep", bufs=1))
         ring = ctx.enter_context(tc.tile_pool(name="ring", bufs=1))
-        psum = ctx.enter_context(tc.psum_pool(name="psum", bufs=8))
+        psum = ctx.enter_context(tc.psum_pool(name="psum", bufs=1))
 
         offsets = keep.tile([P, S // 16], U16, name="offsets")
 
@@ -69,13 +69,26 @@ def tile_list_karaoke_passage_scorer_kernel(
 
         w1_raw, w2_raw, w3_raw, table = {}, {}, {}, {}
         w1_raw[0, 0] = load_rows("w1_raw00", w1_rows(0, 0))
-        table_scales = load_plane("table_scales", tab_scales, False)
+        table_scales = keep.tile([P, T], U8, name="table_scales", align_bytes=64)
+        nc.vector.memset(table_scales[:].bitcast(I32), 0)
+        nc.sync.dma_start(
+            out=table_scales[0:P:4, :].bitcast(I32), in_=tab_scales.bitcast(I32).rearrange("a q c -> q a c")
+        )
         nc.sync.dma_start(offsets[:], offs)
-        table[0] = load_words("table0", tab_words[0])
-        w1_raw[1, 0] = load_rows("w1_raw10", w1_rows(1, 0))
+        table[1] = load_words("table1", tab_words[1])
+        picked_scales = keep.tile([P, S], U8, name="picked_scales", align_bytes=64)
+        nc.vector.tensor_copy(picked_scales[:], table_scales[:].indirect(offsets[:]))
+        v_plane = keep.tile([P, K_PASSES * S], U8, name="v_plane", align_bytes=64)
+        nc.vector.memset(v_plane[:].bitcast(I32), 0)
+        for q in range(4):
+            nc.sync.dma_start(
+                out=v_plane[32 * q : 32 * q + 4, :].bitcast(I32).rearrange("r (a c) -> r a c", a=K_PASSES),
+                in_=picked_scales[32 * q : 32 * q + 32 : 4, :].bitcast(I32),
+            )
         bias1 = keep.tile([P, H_PASSES, PACK], F32, name="bias1")
         nc.sync.dma_start(out=bias1[:], in_=b1.rearrange("(b p t) -> p b t", p=P, t=PACK))
-        table[1] = load_words("table1", tab_words[1])
+        table[0] = load_words("table0", tab_words[0])
+        w1_raw[1, 0] = load_rows("w1_raw10", w1_rows(1, 0))
         w2_raw[0] = load_rows("w2_raw0", w2[:, 0:PASS])
         xs_plane = load_plane("xs_plane", xs_scales, False)
         xs = load_words("xs", xs_words[0])
@@ -94,35 +107,41 @@ def tile_list_karaoke_passage_scorer_kernel(
         def copy_on(engine):
             return nc.scalar.copy if engine == "scalar" else nc.vector.tensor_copy
 
-        def round_dealt(raw, engine):
-            grouped = ring.tile([P, PACK * P * PACK], BF16, name="grouped", bufs=4, align_bytes=64)
-            copy_on(engine)(
-                out=grouped[:].rearrange("p (t m j) -> p m j t", t=PACK, j=PACK),
-                in_=raw[:].rearrange("p j (m t) -> p m j t", t=PACK),
-            )
-            return grouped
-
-        def round_plain(raw, engine):
-            grouped = ring.tile([P, PACK * P * PACK], BF16, name="grouped", bufs=4, align_bytes=64)
-            copy_on(engine)(
-                out=grouped[:, 0 : N * PACK].rearrange("p (c i j) -> p c j i", i=4, j=PACK),
-                in_=raw[:].rearrange("p j (c i) -> p c j i", i=4),
-            )
-            return grouped
-
-        def quantise(name, grouped, widths):
-            columns = sum(widths)
+        def mx_tiles(name, columns):
             codes = keep.tile([P, columns], U32, name=name + "_codes", align_bytes=64)
             plane = keep.tile([P, columns], U8, name=name + "_plane", align_bytes=64)
-            c0 = 0
-            for width in widths:
-                nc.vector.quantize_mx(
-                    out=codes[:, c0 : c0 + width].bitcast(FP8X4),
-                    scales=plane[:, c0 : c0 + width],
-                    in_=grouped[:, PACK * c0 : PACK * (c0 + width)],
-                )
-                c0 += width
             return codes, plane
+
+        def round_dealt(raw, half, engine):
+            grouped = ring.tile([P, 2 * P * PACK], BF16, name="grouped", bufs=6, align_bytes=64)
+            copy_on(engine)(
+                out=grouped[:].rearrange("p (t m j) -> p m j t", t=2, j=PACK),
+                in_=raw[:].rearrange("p j (m t) -> p m j t", t=PACK)[:, :, :, 2 * half : 2 * half + 2],
+            )
+            return grouped
+
+        def round_plain(raw, c0, columns, engine):
+            grouped = ring.tile([P, 2 * P * PACK], BF16, name="grouped", bufs=6, align_bytes=64)
+            copy_on(engine)(
+                out=grouped[:, 0 : columns * PACK].rearrange("p (c i j) -> p c j i", i=2, j=PACK),
+                in_=raw[:, :, c0 : c0 + columns].rearrange("p j (c i) -> p c j i", i=2),
+            )
+            return grouped
+
+        def quantise(mx, c0, columns, grouped):
+            codes, plane = mx
+            nc.vector.quantize_mx(
+                out=codes[:, c0 : c0 + columns].bitcast(FP8X4),
+                scales=plane[:, c0 : c0 + columns],
+                in_=grouped[:, 0 : PACK * columns],
+            )
+
+        def dealt_weight(name, raw, engines):
+            mx = mx_tiles(name, PASS)
+            halves = [round_dealt(raw, half, engines[half]) for half in range(2)]
+            for half in range(2):
+                quantise(mx, 2 * P * half, 2 * P, halves[half])
+            return mx
 
         def gather(name, dtype, window, u):
             picked = keep.tile([P, BANK], dtype, name=name, align_bytes=64)
@@ -137,13 +156,16 @@ def tile_list_karaoke_passage_scorer_kernel(
                 lhsT=codes[:, col0 : col0 + P].bitcast(FP8X4),
                 lhsT_scale=plane[:, col0 : col0 + P],
                 rhs=v_words[a, u][:].bitcast(FP8X4),
-                rhs_scale=v_plane[u][4 * a : P, :],
+                rhs_scale=v_plane[:, a * S + u * BANK : a * S + (u + 1) * BANK],
                 start=(a == 0),
                 stop=(a == K_PASSES - 1),
             )
 
+        banks_taken = []
+
         def new_bank():
-            return psum.tile([P, BANK], F32, name="bank")
+            banks_taken.append(len(banks_taken))
+            return psum.tile([P, BANK], F32, name="bank%d" % (banks_taken[-1] % 8))
 
         def bound(b, banks):
             expect = ring.tile([P, PACK, BANK], F32, name="expect", bufs=3)
@@ -170,62 +192,26 @@ def tile_list_karaoke_passage_scorer_kernel(
                         stop=True,
                     )
                 nc.vector.tensor_tensor(
-                    out=h_rounded[:, c * BANK : (c + 1) * BANK].rearrange("p (g i t) -> p g t i", i=4, t=PACK),
-                    in0=sung[:].rearrange("p (t g i) -> p g t i", t=PACK, i=4),
-                    in1=expect[:, :, c * CHUNK : (c + 1) * CHUNK].rearrange("p t (g i) -> p g t i", i=4),
+                    out=h_rounded[:, c * BANK : (c + 1) * BANK].rearrange("p (g i t) -> p g t i", i=2, t=PACK),
+                    in0=sung[:].rearrange("p (t g i) -> p g t i", t=PACK, i=2),
+                    in1=expect[:, :, c * CHUNK : (c + 1) * CHUNK].rearrange("p t (g i) -> p g t i", i=2),
                     op=ALU.mult,
                 )
             return h_rounded
 
-        v_words, v_plane, w1_mx, w2_mx, w3_mx, h_mx = {}, {}, {}, {}, {}, {}
-        for u in range(HALVES):
-            v_plane[u] = gather("v_plane%d" % u, U8, table_scales[:], u)
-        w1_mx[0, 0] = quantise("w1_00", round_dealt(w1_raw[0, 0], "scalar"), [PASS])
-        for u in range(HALVES):
-            v_words[0, u] = gather("v_words0%d" % u, U32, table[0][:].bitcast(U32), u)
-        banks = {}
-        for u in range(HALVES):
-            for t in range(PACK):
-                banks[u, t] = new_bank()
-                table_pass(banks[u, t], w1_mx[0, 0], t * P, 0, u)
-        w1_mx[1, 0] = quantise("w1_10", round_dealt(w1_raw[1, 0], "scalar"), [PASS])
-        expect = {}
-        for u in range(HALVES):
-            v_words[1, u] = gather("v_words1%d" % u, U32, table[1][:].bitcast(U32), u)
-            for t in range(PACK):
-                table_pass(banks[u, t], w1_mx[1, 0], t * P, 1, u)
-            expect[0, u] = bound(0, [banks[u, t] for t in range(PACK)])
-        w2_mx[0] = quantise("w2_0", round_dealt(w2_raw[0], "vector"), [PASS])
-        w1_grouped = round_dealt(w1_raw[0, 1], "scalar")
-        h_rounded = times_sung(0, 0, expect[0, 0])
-        w1_mx[0, 1] = quantise("w1_01", w1_grouped, [PASS])
-        h_mx[0, 0] = quantise("h_00", h_rounded, [BANK])
-        w1_grouped = round_dealt(w1_raw[1, 1], "scalar")
-        h_rounded = times_sung(0, 1, expect[0, 1])
-        w1_mx[1, 1] = quantise("w1_11", w1_grouped, [PASS])
-        h_mx[0, 1] = quantise("h_01", h_rounded, [BANK])
-        w2_mx[1] = quantise("w2_1", round_dealt(w2_raw[1], "vector"), [PASS])
-        for u in range(HALVES):
-            for t in range(PACK):
-                banks[u, t] = new_bank()
-                for a in range(K_PASSES):
-                    table_pass(banks[u, t], w1_mx[a, 1], t * P, a, u)
-            expect[1, u] = bound(1, [banks[u, t] for t in range(PACK)])
-        w3_mx[0] = quantise("w3_0", round_plain(w3_raw[0], "vector"), [256, 128])
-        h_rounded = times_sung(1, 0, expect[1, 0])
-        w3_mx[1] = quantise("w3_1", round_plain(w3_raw[1], "scalar"), [256, 128])
-        h_mx[1, 0] = quantise("h_10", h_rounded, [BANK])
-        h_rounded = times_sung(1, 1, expect[1, 1])
-        base = {}
-        for u in range(HALVES):
+        def quantise_h(b, u, h_rounded):
+            h_mx[b, u] = mx_tiles("h_%d%d" % (b, u), BANK)
+            quantise(h_mx[b, u], 0, BANK, h_rounded)
+
+        def baseline(u):
             for n in range(N_TILES):
                 acc = new_bank()
                 for a in range(K_PASSES):
                     table_pass(acc, w3_mx[a], n * P, a, u)
                 base[u, n] = keep.tile([P, BANK], F32, name="base%d%d" % (u, n))
                 nc.scalar.activation(out=base[u, n][:], in_=acc[:], func=ACT.Identity, bias=bias3[:, n : n + 1])
-        h_mx[1, 1] = quantise("h_11", h_rounded, [BANK])
-        for u in range(HALVES):
+
+        def scores(u):
             for n in range(N_TILES):
                 acc = new_bank()
                 for b in range(H_PASSES):
@@ -242,3 +228,46 @@ def tile_list_karaoke_passage_scorer_kernel(
                 score = keep.tile([P, BANK], F32, name="score%d%d" % (u, n))
                 nc.vector.tensor_tensor(out=score[:], in0=acc[:], in1=base[u, n][:], op=ALU.max)
                 nc.sync.dma_start(out=out[n * P : (n + 1) * P, u * BANK : (u + 1) * BANK], in_=score[:])
+
+        v_words, w1_mx, w2_mx, w3_mx, h_mx, expect, base = {}, {}, {}, {}, {}, {}, {}
+
+        def plain_weight(name, raw, engines):
+            mx = mx_tiles(name, N)
+            for (c0, columns), engine in zip(((0, 256), (256, 128)), engines):
+                quantise(mx, c0, columns, round_plain(raw, c0, columns, engine))
+            return mx
+
+        def expected(b, u):
+            banks = [new_bank() for t in range(PACK)]
+            for a in range(K_PASSES):
+                for t in range(PACK):
+                    table_pass(banks[t], w1_mx[a, b], t * P, a, u)
+            return bound(b, banks)
+
+        w1_mx[0, 0] = dealt_weight("w1_00", w1_raw[0, 0], ["scalar", "scalar"])
+        for a in (1, 0):
+            for u in range(HALVES):
+                v_words[a, u] = gather("v_words%d%d" % (a, u), U32, table[a][:].bitcast(U32), u)
+        w1_mx[1, 0] = dealt_weight("w1_10", w1_raw[1, 0], ["vector", "scalar"])
+        for u in range(HALVES):
+            expect[0, u] = expected(0, u)
+        w2_mx[0] = dealt_weight("w2_0", w2_raw[0], ["vector", "vector"])
+        h_rounded = times_sung(0, 0, expect[0, 0])
+        w1_mx[0, 1] = dealt_weight("w1_01", w1_raw[0, 1], ["scalar", "scalar"])
+        quantise_h(0, 0, h_rounded)
+        h_rounded = times_sung(0, 1, expect[0, 1])
+        w1_mx[1, 1] = dealt_weight("w1_11", w1_raw[1, 1], ["scalar", "scalar"])
+        quantise_h(0, 1, h_rounded)
+        expect[1, 0] = expected(1, 0)
+        w2_mx[1] = dealt_weight("w2_1", w2_raw[1], ["vector", "vector"])
+        w3_mx[0] = plain_weight("w3_0", w3_raw[0], ["scalar", "scalar"])
+        expect[1, 1] = expected(1, 1)
+        h_rounded = times_sung(1, 0, expect[1, 0])
+        quantise_h(1, 0, h_rounded)
+        w3_mx[1] = plain_weight("w3_1", w3_raw[1], ["vector", "vector"])
+        h_rounded = times_sung(1, 1, expect[1, 1])
+        baseline(0)
+        baseline(1)
+        quantise_h(1, 1, h_rounded)
+        scores(0)
+        scores(1)

@@ -71,26 +71,34 @@ def tile_list_karaoke_passage_scorer_kernel(
         w1_raw[0, 0] = load_rows("w1_raw00", w1_rows(0, 0))
         table_scales = keep.tile([P, T], U8, name="table_scales", align_bytes=64)
         nc.vector.memset(table_scales[:].bitcast(I32), 0)
-        nc.sync.dma_start(
-            out=table_scales[0:P:4, :].bitcast(I32), in_=tab_scales.bitcast(I32).rearrange("a q c -> q a c")
-        )
+        for a in range(K_PASSES):
+            nc.sync.dma_start(
+                out=table_scales[4 * a : P : 8, :].bitcast(I32),
+                in_=tab_scales[a].bitcast(I32).rearrange("(q r) c -> r q c", r=4),
+            )
         nc.sync.dma_start(offsets[:], offs)
         table[1] = load_words("table1", tab_words[1])
+        w1_raw[1, 0] = load_rows("w1_raw10", w1_rows(1, 0))
         picked_scales = keep.tile([P, S], U8, name="picked_scales", align_bytes=64)
         nc.vector.tensor_copy(picked_scales[:], table_scales[:].indirect(offsets[:]))
         v_plane = keep.tile([P, K_PASSES * S], U8, name="v_plane", align_bytes=64)
         nc.vector.memset(v_plane[:].bitcast(I32), 0)
-        for q in range(4):
+        for r in range(4):
             nc.sync.dma_start(
-                out=v_plane[32 * q : 32 * q + 4, :].bitcast(I32).rearrange("r (a c) -> r a c", a=K_PASSES),
-                in_=picked_scales[32 * q : 32 * q + 32 : 4, :].bitcast(I32),
+                out=v_plane[r:P:32, :].bitcast(I32).rearrange("q (a c) -> q a c", a=K_PASSES),
+                in_=picked_scales[32 * r : 32 * r + 32 : 4, :].bitcast(I32),
             )
         bias1 = keep.tile([P, H_PASSES, PACK], F32, name="bias1")
-        nc.sync.dma_start(out=bias1[:], in_=b1.rearrange("(b p t) -> p b t", p=P, t=PACK))
+        nc.gpsimd.dma_start(out=bias1[:], in_=b1.rearrange("(b p t) -> p b t", p=P, t=PACK))
         table[0] = load_words("table0", tab_words[0])
-        w1_raw[1, 0] = load_rows("w1_raw10", w1_rows(1, 0))
         w2_raw[0] = load_rows("w2_raw0", w2[:, 0:PASS])
-        xs_plane = load_plane("xs_plane", xs_scales, False)
+        xs_plane = keep.tile([P, S], U8, name="xs_plane", align_bytes=64)
+        nc.vector.memset(xs_plane[:].bitcast(I32), 0)
+        for q in range(4):
+            nc.gpsimd.dma_start(
+                out=xs_plane[32 * q + 4 : 32 * q + 8, :].bitcast(I32),
+                in_=xs_scales[0, 4 * q : 4 * q + 4, :].bitcast(I32),
+            )
         xs = load_words("xs", xs_words[0])
         w1_raw[0, 1] = load_rows("w1_raw01", w1_rows(0, 1))
         w1_raw[1, 1] = load_rows("w1_raw11", w1_rows(1, 1))
@@ -149,7 +157,7 @@ def tile_list_karaoke_passage_scorer_kernel(
             nc.vector.tensor_copy(picked[:], window.indirect(offsets[:, u * columns : (u + 1) * columns]))
             return picked
 
-        def table_pass(acc, weight, col0, a, u):
+        def table_pass(acc, weight, col0, a, u, order):
             codes, plane = weight
             nc.tensor.matmul_mx(
                 out=acc[:],
@@ -157,8 +165,8 @@ def tile_list_karaoke_passage_scorer_kernel(
                 lhsT_scale=plane[:, col0 : col0 + P],
                 rhs=v_words[a, u][:].bitcast(FP8X4),
                 rhs_scale=v_plane[:, a * S + u * BANK : a * S + (u + 1) * BANK],
-                start=(a == 0),
-                stop=(a == K_PASSES - 1),
+                start=(a == order[0]),
+                stop=(a == order[-1]),
             )
 
         banks_taken = []
@@ -177,7 +185,7 @@ def tile_list_karaoke_passage_scorer_kernel(
 
         def times_sung(b, u, expect):
             codes, plane = w2_mx[b]
-            h_rounded = ring.tile([P, BANK * PACK], BF16, name="h_rounded", bufs=2, align_bytes=64)
+            h_rounded = ring.tile([P, BANK * PACK], BF16, name="h_rounded", bufs=3, align_bytes=64)
             for c in range(PACK):
                 sung = new_bank()
                 s0 = u * BANK + c * CHUNK
@@ -187,7 +195,7 @@ def tile_list_karaoke_passage_scorer_kernel(
                         lhsT=codes[:, t * P : (t + 1) * P].bitcast(FP8X4),
                         lhsT_scale=plane[:, t * P : (t + 1) * P],
                         rhs=xs[:, s0 : s0 + CHUNK].bitcast(FP8X4),
-                        rhs_scale=xs_plane[:, s0 : s0 + CHUNK],
+                        rhs_scale=xs_plane[4:P, s0 : s0 + CHUNK],
                         start=True,
                         stop=True,
                     )
@@ -203,33 +211,68 @@ def tile_list_karaoke_passage_scorer_kernel(
             h_mx[b, u] = mx_tiles("h_%d%d" % (b, u), BANK)
             quantise(h_mx[b, u], 0, BANK, h_rounded)
 
-        def baseline(u):
-            for n in range(N_TILES):
-                acc = new_bank()
-                for a in range(K_PASSES):
-                    table_pass(acc, w3_mx[a], n * P, a, u)
-                base[u, n] = keep.tile([P, BANK], F32, name="base%d%d" % (u, n))
-                nc.scalar.activation(out=base[u, n][:], in_=acc[:], func=ACT.Identity, bias=bias3[:, n : n + 1])
+        def base_sum(u, n):
+            acc = new_bank()
+            for a in range(K_PASSES):
+                table_pass(acc, w3_mx[a], n * P, a, u, (0, 1))
+            return acc
 
-        def scores(u):
+        def y_sum(u, n):
+            acc = new_bank()
+            for b in range(H_PASSES):
+                codes, plane = h_mx[b, u]
+                nc.tensor.matmul_mx(
+                    out=acc[:],
+                    lhsT=w4[:, b, 2 * n * P : 2 * (n + 1) * P].bitcast(FP4X4),
+                    lhsT_scale=w4_plane[:, b * N + n * P : b * N + (n + 1) * P],
+                    rhs=codes[:].bitcast(FP8X4),
+                    rhs_scale=plane[:],
+                    start=(b == 0),
+                    stop=(b == H_PASSES - 1),
+                )
+            return acc
+
+        def park_y(u):
             for n in range(N_TILES):
-                acc = new_bank()
-                for b in range(H_PASSES):
-                    codes, plane = h_mx[b, u]
-                    nc.tensor.matmul_mx(
-                        out=acc[:],
-                        lhsT=w4[:, b, 2 * n * P : 2 * (n + 1) * P].bitcast(FP4X4),
-                        lhsT_scale=w4_plane[:, b * N + n * P : b * N + (n + 1) * P],
-                        rhs=codes[:].bitcast(FP8X4),
-                        rhs_scale=plane[:],
-                        start=(b == 0),
-                        stop=(b == H_PASSES - 1),
-                    )
+                parked[u, n] = keep.tile([P, BANK], F32, name="parked%d%d" % (u, n))
+                nc.scalar.copy(out=parked[u, n][:], in_=y_sum(u, n)[:])
+
+        def park_base(u):
+            for n in range(N_TILES):
+                parked[u, n] = keep.tile([P, BANK], F32, name="parked%d%d" % (u, n))
+                nc.scalar.activation(
+                    out=parked[u, n][:], in_=base_sum(u, n)[:], func=ACT.Identity, bias=bias3[:, n : n + 1]
+                )
+
+        def store(u, n, cols, score):
+            nc.sync.dma_start(
+                out=out[n * P : (n + 1) * P, u * BANK + cols.start : u * BANK + cols.stop], in_=score[:, cols]
+            )
+
+        def scores_from_base(u):
+            for n in range(N_TILES):
                 score = keep.tile([P, BANK], F32, name="score%d%d" % (u, n))
-                nc.vector.tensor_tensor(out=score[:], in0=acc[:], in1=base[u, n][:], op=ALU.max)
-                nc.sync.dma_start(out=out[n * P : (n + 1) * P, u * BANK : (u + 1) * BANK], in_=score[:])
+                nc.vector.scalar_tensor_tensor(
+                    out=score[:],
+                    in0=base_sum(u, n)[:],
+                    scalar=bias3[:, n : n + 1],
+                    in1=parked[u, n][:],
+                    op0=ALU.add,
+                    op1=ALU.max,
+                )
+                store(u, n, slice(0, BANK), score)
 
-        v_words, w1_mx, w2_mx, w3_mx, h_mx, expect, base = {}, {}, {}, {}, {}, {}, {}
+        def scores_from_y(u):
+            for n in range(N_TILES):
+                acc = y_sum(u, n)
+                score = keep.tile([P, BANK], F32, name="score%d%d" % (u, n))
+                pieces = 2 if n == N_TILES - 1 else 1
+                for piece in range(pieces):
+                    cols = slice(piece * BANK // pieces, (piece + 1) * BANK // pieces)
+                    nc.vector.tensor_tensor(out=score[:, cols], in0=acc[:, cols], in1=parked[u, n][:, cols], op=ALU.max)
+                    store(u, n, cols, score)
+
+        v_words, w1_mx, w2_mx, w3_mx, h_mx, expect, parked = {}, {}, {}, {}, {}, {}, {}
 
         def plain_weight(name, raw, engines):
             mx = mx_tiles(name, N)
@@ -237,37 +280,37 @@ def tile_list_karaoke_passage_scorer_kernel(
                 quantise(mx, c0, columns, round_plain(raw, c0, columns, engine))
             return mx
 
-        def expected(b, u):
+        def expected(b, u, order):
             banks = [new_bank() for t in range(PACK)]
-            for a in range(K_PASSES):
+            for a in order:
                 for t in range(PACK):
-                    table_pass(banks[t], w1_mx[a, b], t * P, a, u)
+                    table_pass(banks[t], w1_mx[a, b], t * P, a, u, order)
             return bound(b, banks)
 
         w1_mx[0, 0] = dealt_weight("w1_00", w1_raw[0, 0], ["scalar", "scalar"])
+        w1_mx[1, 0] = dealt_weight("w1_10", w1_raw[1, 0], ["scalar", "scalar"])
         for a in (1, 0):
             for u in range(HALVES):
                 v_words[a, u] = gather("v_words%d%d" % (a, u), U32, table[a][:].bitcast(U32), u)
-        w1_mx[1, 0] = dealt_weight("w1_10", w1_raw[1, 0], ["vector", "scalar"])
         for u in range(HALVES):
-            expect[0, u] = expected(0, u)
+            expect[0, u] = expected(0, u, (1, 0))
         w2_mx[0] = dealt_weight("w2_0", w2_raw[0], ["vector", "vector"])
-        h_rounded = times_sung(0, 0, expect[0, 0])
+        h00 = times_sung(0, 0, expect[0, 0])
         w1_mx[0, 1] = dealt_weight("w1_01", w1_raw[0, 1], ["scalar", "scalar"])
-        quantise_h(0, 0, h_rounded)
-        h_rounded = times_sung(0, 1, expect[0, 1])
         w1_mx[1, 1] = dealt_weight("w1_11", w1_raw[1, 1], ["scalar", "scalar"])
-        quantise_h(0, 1, h_rounded)
-        expect[1, 0] = expected(1, 0)
+        h01 = times_sung(0, 1, expect[0, 1])
+        expect[1, 0] = expected(1, 0, (0, 1))
         w2_mx[1] = dealt_weight("w2_1", w2_raw[1], ["vector", "vector"])
+        quantise_h(0, 0, h00)
+        quantise_h(0, 1, h01)
         w3_mx[0] = plain_weight("w3_0", w3_raw[0], ["scalar", "scalar"])
-        expect[1, 1] = expected(1, 1)
-        h_rounded = times_sung(1, 0, expect[1, 0])
-        quantise_h(1, 0, h_rounded)
-        w3_mx[1] = plain_weight("w3_1", w3_raw[1], ["vector", "vector"])
-        h_rounded = times_sung(1, 1, expect[1, 1])
-        baseline(0)
-        baseline(1)
-        quantise_h(1, 1, h_rounded)
-        scores(0)
-        scores(1)
+        expect[1, 1] = expected(1, 1, (0, 1))
+        w3_mx[1] = plain_weight("w3_1", w3_raw[1], ["scalar", "scalar"])
+        h10 = times_sung(1, 0, expect[1, 0])
+        quantise_h(1, 0, h10)
+        h11 = times_sung(1, 1, expect[1, 1])
+        park_y(0)
+        quantise_h(1, 1, h11)
+        scores_from_base(0)
+        park_base(1)
+        scores_from_y(1)

@@ -71,11 +71,9 @@ def tile_list_karaoke_passage_scorer_kernel(
         w1_raw[0, 0] = load_rows("w1_raw00", w1_rows(0, 0))
         table_scales = keep.tile([P, T], U8, name="table_scales", align_bytes=64)
         nc.vector.memset(table_scales[:].bitcast(I32), 0)
-        for a in range(K_PASSES):
-            nc.sync.dma_start(
-                out=table_scales[4 * a : P : 8, :].bitcast(I32),
-                in_=tab_scales[a].bitcast(I32).rearrange("(q r) c -> r q c", r=4),
-            )
+        nc.sync.dma_start(
+            out=table_scales[0:P:4, :].bitcast(I32), in_=tab_scales.bitcast(I32).rearrange("a q c -> q a c")
+        )
         nc.sync.dma_start(offsets[:], offs)
         table[1] = load_words("table1", tab_words[1])
         w1_raw[1, 0] = load_rows("w1_raw10", w1_rows(1, 0))
@@ -83,21 +81,20 @@ def tile_list_karaoke_passage_scorer_kernel(
         nc.vector.tensor_copy(picked_scales[:], table_scales[:].indirect(offsets[:]))
         v_plane = keep.tile([P, K_PASSES * S], U8, name="v_plane", align_bytes=64)
         nc.vector.memset(v_plane[:].bitcast(I32), 0)
-        for r in range(4):
+        for q in range(4):
             nc.sync.dma_start(
-                out=v_plane[r:P:32, :].bitcast(I32).rearrange("q (a c) -> q a c", a=K_PASSES),
-                in_=picked_scales[32 * r : 32 * r + 32 : 4, :].bitcast(I32),
+                out=v_plane[32 * q : 32 * q + 4, :].bitcast(I32).rearrange("r (a c) -> r a c", a=K_PASSES),
+                in_=picked_scales[32 * q : 32 * q + 32 : 4, :].bitcast(I32),
             )
         bias1 = keep.tile([P, H_PASSES, PACK], F32, name="bias1")
-        nc.gpsimd.dma_start(out=bias1[:], in_=b1.rearrange("(b p t) -> p b t", p=P, t=PACK))
+        nc.sync.dma_start(out=bias1[:], in_=b1.rearrange("(b p t) -> p b t", p=P, t=PACK))
         table[0] = load_words("table0", tab_words[0])
         w2_raw[0] = load_rows("w2_raw0", w2[:, 0:PASS])
         xs_plane = keep.tile([P, S], U8, name="xs_plane", align_bytes=64)
         nc.vector.memset(xs_plane[:].bitcast(I32), 0)
-        for q in range(4):
-            nc.gpsimd.dma_start(
-                out=xs_plane[32 * q + 4 : 32 * q + 8, :].bitcast(I32),
-                in_=xs_scales[0, 4 * q : 4 * q + 4, :].bitcast(I32),
+        for r in range(4):
+            nc.sync.dma_start(
+                out=xs_plane[4 + r : P : 32, :].bitcast(I32), in_=xs_scales[0, r:16:4, :].bitcast(I32)
             )
         xs = load_words("xs", xs_words[0])
         w1_raw[0, 1] = load_rows("w1_raw01", w1_rows(0, 1))
@@ -131,8 +128,8 @@ def tile_list_karaoke_passage_scorer_kernel(
         def round_plain(raw, c0, columns, engine):
             grouped = ring.tile([P, 2 * P * PACK], BF16, name="grouped", bufs=6, align_bytes=64)
             copy_on(engine)(
-                out=grouped[:, 0 : columns * PACK].rearrange("p (c i j) -> p c j i", i=2, j=PACK),
-                in_=raw[:, :, c0 : c0 + columns].rearrange("p j (c i) -> p c j i", i=2),
+                out=grouped[:, 0 : columns * PACK].rearrange("p (c i j) -> p c j i", i=4, j=PACK),
+                in_=raw[:, :, c0 : c0 + columns].rearrange("p j (c i) -> p c j i", i=4),
             )
             return grouped
 
@@ -296,7 +293,7 @@ def tile_list_karaoke_passage_scorer_kernel(
             expect[0, u] = expected(0, u, (1, 0))
         w2_mx[0] = dealt_weight("w2_0", w2_raw[0], ["vector", "vector"])
         h00 = times_sung(0, 0, expect[0, 0])
-        w1_mx[0, 1] = dealt_weight("w1_01", w1_raw[0, 1], ["scalar", "scalar"])
+        w1_mx[0, 1] = dealt_weight("w1_01", w1_raw[0, 1], ["vector", "scalar"])
         w1_mx[1, 1] = dealt_weight("w1_11", w1_raw[1, 1], ["scalar", "scalar"])
         h01 = times_sung(0, 1, expect[0, 1])
         expect[1, 0] = expected(1, 0, (0, 1))

from contextlib import ExitStack

import concourse.mybir as mybir

K, K2, H, N, T, S = 1024, 512, 1024, 384, 4096, 1024
FLOPS = 2 * S * (K * H + K2 * H + H * N + K * N)

F32 = mybir.dt.float32
BF16 = mybir.dt.bfloat16
I32 = mybir.dt.int32
U32 = mybir.dt.uint32
U16 = mybir.dt.uint16
U8 = mybir.dt.uint8
FP8X4 = mybir.dt.float8_e4m3fn_x4
FP4X4 = mybir.dt.float4_e2m1fn_x4
ACT = mybir.ActivationFunctionType
ALU = mybir.AluOpType

P = 128
PACK = 4
PASS = P * PACK
BANK = 512
HALVES = S // BANK
K_PASSES = K // PASS
H_PASSES = H // PASS
N_TILES = N // P
CHUNK = BANK // PACK


def tile_list_karaoke_passage_scorer_kernel(
    tc, tab_words, tab_scales, offs, xs_words, xs_scales, w1, b1, w2, w3, b3, w4_words, w4_scales, out
):
    nc = tc.nc
    with ExitStack() as ctx:
        keep = ctx.enter_context(tc.tile_pool(name="keep", bufs=1))
        ring = ctx.enter_context(tc.tile_pool(name="ring", bufs=1))
        psum = ctx.enter_context(tc.psum_pool(name="psum", bufs=1))

        offsets = keep.tile([P, S // 16], U16, name="offsets")

        def load_rows(name, rows):
            width = rows.shape[1]
            raw = keep.tile([P, PACK, width], F32, name=name)
            nc.sync.dma_start(out=raw[:], in_=rows.rearrange("(p j) w -> p j w", j=PACK))
            return raw

        def load_words(name, words):
            tile = keep.tile([P, words.shape[1]], I32, name=name, align_bytes=64)
            nc.sync.dma_start(out=tile[:], in_=words.rearrange("p c i -> p (c i)").bitcast(I32))
            return tile

        def w1_rows(a, b):
            return w1[a * PASS : (a + 1) * PASS, b * PASS : (b + 1) * PASS]

        def load_plane(name, scales, side_by_side):
            passes, width = scales.shape[0], scales.shape[2]
            plane = keep.tile([P, passes * width if side_by_side else width], U8, name=name, align_bytes=64)
            nc.vector.memset(plane[:].bitcast(I32), 0)
            for q in range(4):
                rows = scales[:, 4 * q : 4 * q + 4, :].bitcast(I32)
                if side_by_side:
                    nc.sync.dma_start(
                        out=plane[32 * q : 32 * q + 4, :].bitcast(I32).rearrange("r (b c) -> r b c", b=passes),
                        in_=rows.rearrange("b r c -> r b c"),
                    )
                else:
                    nc.sync.dma_start(out=plane[32 * q : 32 * q + 4 * passes, :].bitcast(I32), in_=rows)
            return plane

        w1_raw, w2_raw, w3_raw, table = {}, {}, {}, {}
        w1_raw[0, 0] = load_rows("w1_raw00", w1_rows(0, 0))
        table_scales = keep.tile([P, T], U8, name="table_scales", align_bytes=64)
        nc.vector.memset(table_scales[:].bitcast(I32), 0)
        nc.sync.dma_start(
            out=table_scales[0:P:4, :].bitcast(I32), in_=tab_scales.bitcast(I32).rearrange("a q c -> q a c")
        )
        nc.sync.dma_start(offsets[:], offs)
        table[1] = load_words("table1", tab_words[1])
        w1_raw[1, 0] = load_rows("w1_raw10", w1_rows(1, 0))
        picked_scales = keep.tile([P, S], U8, name="picked_scales", align_bytes=64)
        nc.vector.tensor_copy(picked_scales[:], table_scales[:].indirect(offsets[:]))
        v_plane = keep.tile([P, K_PASSES * S], U8, name="v_plane", align_bytes=64)
        nc.vector.memset(v_plane[:].bitcast(I32), 0)
        for q in range(4):
            nc.sync.dma_start(
                out=v_plane[32 * q : 32 * q + 4, :].bitcast(I32).rearrange("r (a c) -> r a c", a=K_PASSES),
                in_=picked_scales[32 * q : 32 * q + 32 : 4, :].bitcast(I32),
            )
        bias1 = keep.tile([P, H_PASSES, PACK], F32, name="bias1")
        nc.sync.dma_start(out=bias1[:], in_=b1.rearrange("(b p t) -> p b t", p=P, t=PACK))
        table[0] = load_words("table0", tab_words[0])
        w2_raw[0] = load_rows("w2_raw0", w2[:, 0:PASS])
        xs_plane = keep.tile([P, S], U8, name="xs_plane", align_bytes=64)
        nc.vector.memset(xs_plane[:].bitcast(I32), 0)
        for r in range(4):
            nc.sync.dma_start(
                out=xs_plane[4 + r : P : 32, :].bitcast(I32), in_=xs_scales[0, r:16:4, :].bitcast(I32)
            )
        xs = load_words("xs", xs_words[0])
        w1_raw[0, 1] = load_rows("w1_raw01", w1_rows(0, 1))
        w1_raw[1, 1] = load_rows("w1_raw11", w1_rows(1, 1))
        w2_raw[1] = load_rows("w2_raw1", w2[:, PASS : 2 * PASS])
        for a in range(K_PASSES):
            w3_raw[a] = load_rows("w3_raw%d" % a, w3[a * PASS : (a + 1) * PASS, :])
        bias3 = keep.tile([P, N_TILES], F32, name="bias3")
        with nc.allow_non_contiguous_dma(reason="one bias value to a partition"):
            nc.sync.dma_start(out=bias3[:], in_=b3.rearrange("(c p) -> p c", p=P))
        w4 = keep.tile([P, H_PASSES, 2 * N], U8, name="w4", align_bytes=64)
        nc.sync.dma_start(out=w4[:].bitcast(I32), in_=w4_words.bitcast(I32).rearrange("b p c -> p b c"))
        w4_plane = load_plane("w4_plane", w4_scales, True)

        def copy_on(engine):
            return nc.scalar.copy if engine == "scalar" else nc.vector.tensor_copy

        def mx_tiles(name, columns):
            codes = keep.tile([P, columns], U32, name=name + "_codes", align_bytes=64)
            plane = keep.tile([P, columns], U8, name=name + "_plane", align_bytes=64)
            return codes, plane

        def round_dealt(raw, half, engine):
            grouped = ring.tile([P, 2 * P * PACK], BF16, name="grouped", bufs=6, align_bytes=64)
            copy_on(engine)(
                out=grouped[:].rearrange("p (t m j) -> p m j t", t=2, j=PACK),
                in_=raw[:].rearrange("p j (m t) -> p m j t", t=PACK)[:, :, :, 2 * half : 2 * half + 2],
            )
            return grouped

        def round_plain(raw, c0, columns, engine):
            grouped = ring.tile([P, 2 * P * PACK], BF16, name="grouped", bufs=6, align_bytes=64)
            copy_on(engine)(
                out=grouped[:, 0 : columns * PACK].rearrange("p (c i j) -> p c j i", i=4, j=PACK),
                in_=raw[:, :, c0 : c0 + columns].rearrange("p j (c i) -> p c j i", i=4),
            )
            return grouped

        def quantise(mx, c0, columns, grouped):
            codes, plane = mx
            nc.vector.quantize_mx(
                out=codes[:, c0 : c0 + columns].bitcast(FP8X4),
                scales=plane[:, c0 : c0 + columns],
                in_=grouped[:, 0 : PACK * columns],
            )

        def dealt_weight(name, raw, engines):
            mx = mx_tiles(name, PASS)
            halves = [round_dealt(raw, half, engines[half]) for half in range(2)]
            for half in range(2):
                quantise(mx, 2 * P * half, 2 * P, halves[half])
            return mx

        def gather(name, dtype, window, u):
            picked = keep.tile([P, BANK], dtype, name=name, align_bytes=64)
            columns = BANK // 16
            nc.vector.tensor_copy(picked[:], window.indirect(offsets[:, u * columns : (u + 1) * columns]))
            return picked

        def table_pass(acc, weight, col0, a, u, order):
            codes, plane = weight
            nc.tensor.matmul_mx(
                out=acc[:],
                lhsT=codes[:, col0 : col0 + P].bitcast(FP8X4),
                lhsT_scale=plane[:, col0 : col0 + P],
                rhs=v_words[a, u][:].bitcast(FP8X4),
                rhs_scale=v_plane[:, a * S + u * BANK : a * S + (u + 1) * BANK],
                start=(a == order[0]),
                stop=(a == order[-1]),
            )

        banks_taken = []

        def new_bank():
            banks_taken.append(len(banks_taken))
            return psum.tile([P, BANK], F32, name="bank%d" % (banks_taken[-1] % 8))

        def bound(b, banks):
            expect = ring.tile([P, PACK, BANK], F32, name="expect", bufs=3)
            for t in range(PACK):
                nc.scalar.activation(
                    out=expect[:, t, :], in_=banks[t][:], func=ACT.Tanh, bias=bias1[:, b, t : t + 1]
                )
            return expect

        def times_sung(b, u, expect):
            codes, plane = w2_mx[b]
            h_rounded = ring.tile([P, BANK * PACK], BF16, name="h_rounded", bufs=3, align_bytes=64)
            for c in range(PACK):
                sung = new_bank()
                s0 = u * BANK + c * CHUNK
                for t in range(PACK):
                    nc.tensor.matmul_mx(
                        out=sung[:, t * CHUNK : (t + 1) * CHUNK],
                        lhsT=codes[:, t * P : (t + 1) * P].bitcast(FP8X4),
                        lhsT_scale=plane[:, t * P : (t + 1) * P],
                        rhs=xs[:, s0 : s0 + CHUNK].bitcast(FP8X4),
                        rhs_scale=xs_plane[4:P, s0 : s0 + CHUNK],
                        start=True,
                        stop=True,
                    )
                nc.vector.tensor_tensor(
                    out=h_rounded[:, c * BANK : (c + 1) * BANK].rearrange("p (g i t) -> p g t i", i=2, t=PACK),
                    in0=sung[:].rearrange("p (t g i) -> p g t i", t=PACK, i=2),
                    in1=expect[:, :, c * CHUNK : (c + 1) * CHUNK].rearrange("p t (g i) -> p g t i", i=2),
                    op=ALU.mult,
                )
            return h_rounded

        def quantise_h(b, u, h_rounded):
            h_mx[b, u] = mx_tiles("h_%d%d" % (b, u), BANK)
            quantise(h_mx[b, u], 0, BANK, h_rounded)

        def base_sum(u, n):
            acc = new_bank()
            for a in range(K_PASSES):
                table_pass(acc, w3_mx[a], n * P, a, u, (0, 1))
            return acc

        def y_sum(u, n):
            acc = new_bank()
            for b in range(H_PASSES):
                codes, plane = h_mx[b, u]
                nc.tensor.matmul_mx(
                    out=acc[:],
                    lhsT=w4[:, b, 2 * n * P : 2 * (n + 1) * P].bitcast(FP4X4),
                    lhsT_scale=w4_plane[:, b * N + n * P : b * N + (n + 1) * P],
                    rhs=codes[:].bitcast(FP8X4),
                    rhs_scale=plane[:],
                    start=(b == 0),
                    stop=(b == H_PASSES - 1),
                )
            return acc

        def park_y(u):
            for n in range(N_TILES):
                parked[u, n] = keep.tile([P, BANK], F32, name="parked%d%d" % (u, n))
                nc.scalar.copy(out=parked[u, n][:], in_=y_sum(u, n)[:])

        def park_base(u):
            for n in range(N_TILES):
                parked[u, n] = keep.tile([P, BANK], F32, name="parked%d%d" % (u, n))
                nc.scalar.activation(
                    out=parked[u, n][:], in_=base_sum(u, n)[:], func=ACT.Identity, bias=bias3[:, n : n + 1]
                )

        def store(u, n, cols, score):
            nc.sync.dma_start(
                out=out[n * P : (n + 1) * P, u * BANK + cols.start : u * BANK + cols.stop], in_=score[:, cols]
            )

        def scores_from_base(u):
            for n in range(N_TILES):
                score = keep.tile([P, BANK], F32, name="score%d%d" % (u, n))
                nc.vector.scalar_tensor_tensor(
                    out=score[:],
                    in0=base_sum(u, n)[:],
                    scalar=bias3[:, n : n + 1],
                    in1=parked[u, n][:],
                    op0=ALU.add,
                    op1=ALU.max,
                )
                store(u, n, slice(0, BANK), score)

        def scores_from_y(u):
            for n in range(N_TILES):
                acc = y_sum(u, n)
                score = keep.tile([P, BANK], F32, name="score%d%d" % (u, n))
                pieces = 2 if n == N_TILES - 1 else 1
                for piece in range(pieces):
                    cols = slice(piece * BANK // pieces, (piece + 1) * BANK // pieces)
                    nc.vector.tensor_tensor(out=score[:, cols], in0=acc[:, cols], in1=parked[u, n][:, cols], op=ALU.max)
                    store(u, n, cols, score)

        v_words, w1_mx, w2_mx, w3_mx, h_mx, expect, parked = {}, {}, {}, {}, {}, {}, {}

        def plain_weight(name, raw, engines):
            mx = mx_tiles(name, N)
            for (c0, columns), engine in zip(((0, 256), (256, 128)), engines):
                quantise(mx, c0, columns, round_plain(raw, c0, columns, engine))
            return mx

        def expected(b, u, order):
            banks = [new_bank() for t in range(PACK)]
            for a in order:
                for t in range(PACK):
                    table_pass(banks[t], w1_mx[a, b], t * P, a, u, order)
            return bound(b, banks)

        w1_mx[0, 0] = dealt_weight("w1_00", w1_raw[0, 0], ["scalar", "scalar"])
        w1_mx[1, 0] = dealt_weight("w1_10", w1_raw[1, 0], ["scalar", "scalar"])
        for a in (1, 0):
            for u in range(HALVES):
                v_words[a, u] = gather("v_words%d%d" % (a, u), U32, table[a][:].bitcast(U32), u)
        for u in range(HALVES):
            expect[0, u] = expected(0, u, (1, 0))
        w2_mx[0] = dealt_weight("w2_0", w2_raw[0], ["vector", "vector"])
        h00 = times_sung(0, 0, expect[0, 0])
        w1_mx[0, 1] = dealt_weight("w1_01", w1_raw[0, 1], ["vector", "scalar"])
        w1_mx[1, 1] = dealt_weight("w1_11", w1_raw[1, 1], ["scalar", "scalar"])
        h01 = times_sung(0, 1, expect[0, 1])
        expect[1, 0] = expected(1, 0, (0, 1))
        w2_mx[1] = dealt_weight("w2_1", w2_raw[1], ["vector", "vector"])
        quantise_h(0, 0, h00)
        quantise_h(0, 1, h01)
        w3_mx[0] = plain_weight("w3_0", w3_raw[0], ["scalar", "scalar"])
        expect[1, 1] = expected(1, 1, (0, 1))
        w3_mx[1] = plain_weight("w3_1", w3_raw[1], ["scalar", "scalar"])
        h10 = times_sung(1, 0, expect[1, 0])
        quantise_h(1, 0, h10)
        h11 = times_sung(1, 1, expect[1, 1])
        park_y(0)
        quantise_h(1, 1, h11)
        scores_from_base(0)
        park_base(1)
        scores_from_y(1)
